import numpy as np
import ml_dtypes


def mxq(x, axis, fmt="e4m3"):
    dtype, down = {"e4m3": (ml_dtypes.float8_e4m3fn, 7), "e5m2": (ml_dtypes.float8_e5m2, 14)}[fmt]
    v = np.moveaxis(np.asarray(x, np.float32).astype(ml_dtypes.bfloat16).astype(np.float64), axis, -1)
    blocks = v.reshape(v.shape[:-1] + (-1, 32))
    amax = np.abs(blocks).max(-1, keepdims=True)
    byte = np.maximum(np.where(amax > 0, np.frexp(amax)[1] - 1 + 127, 0) - down, 1)
    scale = np.exp2(byte - 127.0)
    codes = (blocks / scale).astype(np.float32).astype(dtype).astype(np.float64)
    return np.moveaxis((codes * scale).reshape(v.shape), -1, axis)


WIDE = False


def mx_kscale(k):
    if not WIDE:
        return np.ones(k)
    levels = np.array([10, -10, 5, -5, 0])
    if k % 512:
        return np.exp2(np.random.permutation(np.resize(levels, k // 32))).repeat(32)
    a = np.empty((k // 512, 16))
    for p in range(k // 512):
        a[p, :8] = np.random.permutation(np.resize(levels, 8))
        for g in range(8):
            far = levels[np.abs(levels - a[p, g]) >= 10]
            a[p, g + 8] = far[np.random.randint(len(far))]
    return np.exp2(a.ravel()).repeat(32)


def f64(x):
    return np.asarray(x).astype(np.float64)


def striped(idx):
    return np.tile(idx.reshape(-1, 16).T, (8, 1)).astype(np.uint16)


def unstriped(offs):
    return offs[:16].T.reshape(-1).astype(np.int64)


E2M1 = np.array([0.0, 0.5, 1.0, 1.5, 2.0, 3.0, 4.0, 6.0, -0.0, -0.5, -1.0, -1.5, -2.0, -3.0, -4.0, -6.0])


def pack_weight(w, fmt):
    k, n = w.shape
    w = f64(np.asarray(w, np.float32).astype(ml_dtypes.bfloat16)).reshape(k // 32, 32, n)
    amax = np.abs(w).max(1)
    if fmt == "e4m3":
        byte = np.frexp(amax)[1] - 1 + 127 - 7
    else:
        mant, ex = np.frexp(amax / 6.0)
        byte = np.where(mant > 0.5, ex, ex - 1) + 127
    byte = np.clip(np.where(amax > 0, byte, 1), 1, 254)
    scaled = (w * np.exp2(127.0 - byte)[:, None, :]).reshape(k, n).astype(np.float32)
    by_word = np.ascontiguousarray(scaled.reshape(k // 512, 128, 4, n).transpose(0, 1, 3, 2))
    if fmt == "e4m3":
        words = by_word.astype(ml_dtypes.float8_e4m3fn).view(np.uint8)
    else:
        c = by_word.astype(ml_dtypes.float4_e2m1fn).view(np.uint8) & 0xF
        words = (c[..., 0::2] | (c[..., 1::2] << 4)).reshape(k // 512, 128, 2 * n)
    return np.ascontiguousarray(words), np.ascontiguousarray(byte.astype(np.uint8).reshape(k // 512, 16, n))


def unpack_weight(words, scales, fmt):
    g, _, n = scales.shape
    words = np.ascontiguousarray(words).reshape(g, 128, n, -1)
    if fmt == "e4m3":
        vals = words.view(ml_dtypes.float8_e4m3fn).astype(np.float64)
    else:
        nib = np.empty((g, 128, n, 4), np.uint8)
        nib[..., 0::2] = words & 0xF
        nib[..., 1::2] = words >> 4
        vals = E2M1[nib]
    vals = vals * np.repeat(np.exp2(scales.astype(np.float64) - 127.0), 8, axis=1)[..., None]
    return vals.transpose(0, 1, 3, 2).reshape(g * 512, n)


def gelu(v):
    return 0.5 * v * (1.0 + np.tanh(np.sqrt(2.0 / np.pi) * (v + 0.044715 * v**3)))


def striped8(idx):
    return np.concatenate([v.reshape(-1, 16).T for v in idx]).astype(np.uint16)


def unstriped8(offs):
    return np.stack([offs[16 * g:16 * g + 16].T.reshape(-1) for g in range(8)]).astype(np.int64)


def heads(h, wgt, idx8):
    r = np.arange(h.shape[0])
    return wgt[r // 4 % 128] * h[r[:, None], idx8[r % 512 // 64]]


K, T, S, H, T2, P, N = 1024, 2048, 1024, 512, 2048, 1024, 768

def setup_inputs():
    n = np.random.standard_normal
    s = mx_kscale(K)[:, None]
    u = mx_kscale(H)[:, None]
    tab_words, tab_scales = pack_weight(n((K, T)) * s, "e4m3")
    w3_words, w3_scales = pack_weight(0.6 * n((K, H)) / np.sqrt(K) / s * u.T, "e2m1")
    w4_words, w4_scales = pack_weight(n((H, N)) / np.sqrt(H) / u, "e4m3")
    eight = np.stack([np.random.permutation(T2)[:P] for _ in range(8)])
    return {
        "tab_words": tab_words, "tab_scales": tab_scales,
        "offs": striped(np.random.permutation(T)[:S]),
        "offs2": striped(np.random.permutation(T2)[:S]),
        "offs3": striped8(eight),
        "w1": (1.3 * n((K, H)) / np.sqrt(K) / s).astype(np.float32),
        "w2": (0.38 * n((K, H)) / np.sqrt(K) / s).astype(np.float32),
        "b2": np.random.uniform(-0.8, 0.8, H).astype(np.float32),
        "gain": (1.2 * np.exp(0.3 * n(H)) * u[:, 0]).astype(np.float32),
        "w3_words": w3_words, "w3_scales": w3_scales,
        "page0": (n((H, T2)) * u).astype(np.float32),
        "wgs": np.exp(0.3 * n((128, S))).astype(np.float32),
        "wgt": np.repeat(np.random.uniform(0.5, 2.0, (8, P)), 16, axis=0).astype(np.float32),
        "w4_words": w4_words, "w4_scales": w4_scales,
    }

def reference(tab_words, tab_scales, offs, offs2, offs3, w1, w2, b2, gain, w3_words, w3_scales, page0, wgs, wgt, w4_words, w4_scales):
    v = unpack_weight(tab_words, tab_scales, "e4m3")[:, unstriped(offs)]
    w3 = unpack_weight(w3_words, w3_scales, "e2m1")
    w4 = unpack_weight(w4_words, w4_scales, "e4m3")
    slip = np.tanh(mxq(f64(w1), 0, "e4m3").T @ v)
    lean = np.cos((mxq(f64(w2), 0, "e4m3").T @ v) + f64(b2)[:, None])
    load = w3.T @ v
    h = f64(gain)[:, None] * slip * lean + load
    page = f64(page0).copy()
    page[:, unstriped(offs2)] = np.tile(f64(wgs), (H // 128, 1)) * h
    x = heads(page, f64(wgt), unstriped8(offs3))
    out = w4.T @ mxq(x, 0, "e4m3")
    return out

@@ -1,0 +1,257 @@
+import math
+from contextlib import ExitStack
+
+import concourse.mybir as mybir
+
+K, T, S, H, T2, M, N = 1024, 2048, 1024, 512, 2048, 1024, 768
+FLOPS = 2 * (3 * K * H * S + H * N * M)
+
+F32 = mybir.dt.float32
+BF16 = mybir.dt.bfloat16
+I32 = mybir.dt.int32
+U32 = mybir.dt.uint32
+U16 = mybir.dt.uint16
+U8 = mybir.dt.uint8
+FP8X4 = mybir.dt.float8_e4m3fn_x4
+FP4X4 = mybir.dt.float4_e2m1fn_x4
+ACT = mybir.ActivationFunctionType
+ALU = mybir.AluOpType
+
+P = 128
+PACK = 4
+PASSES = K // (P * PACK)
+HALF = 512
+TWO_PI = 2.0 * math.pi
+ROUNDER = 1.5 * 2.0**23
+CHUNKS = (128, 128, 256, 256, 128, 128)
+
+
+def tile_list_lean_grip_features_kernel(
+    tc, tab_words, tab_scales, offs, offs2, offs3, w1, w2, b2, gain, w3_words, w3_scales,
+    page0, wgs, wgt, w4_words, w4_scales, out,
+):
+    nc = tc.nc
+    with ExitStack() as ctx:
+        keep = ctx.enter_context(tc.tile_pool(name="keep", bufs=1))
+        ring = ctx.enter_context(tc.tile_pool(name="ring", bufs=3))
+        psum = ctx.enter_context(tc.psum_pool(name="psum", bufs=1))
+
+        def held(shape, dtype, name, tag=""):
+            return keep.tile(shape, dtype, name=name, tag=tag or name, align_bytes=64)
+
+        def load_scale_rows(queue, plane, scales):
+            passes = scales.shape[0]
+            for q in range(4):
+                queue.dma_start(
+                    out=plane[32 * q : 32 * q + 4, :].bitcast(I32).rearrange("r (a c) -> r a c", a=passes),
+                    in_=scales[:, 4 * q : 4 * q + 4, :].bitcast(I32).rearrange("a r c -> r a c"),
+                )
+
+        list1 = keep.tile([P, S // 16], U16, name="list1")
+        list2 = keep.tile([P, S // 16], U16, name="list2")
+        list3 = keep.tile([P, M // 16], U16, name="list3")
+
+        tab_plane = held([P, PASSES * T], U8, "tab_plane")
+        w3_plane_raw = held([P, PASSES * H], U8, "w3_plane_raw")
+        w4_plane = held([P, N], U8, "w4_plane")
+        for plane in (tab_plane, w3_plane_raw, w4_plane):
+            nc.vector.memset(plane[:].bitcast(I32), 0)
+
+        nc.sync.dma_start(list1[:], offs)
+        w3_raw = held([P, PASSES * 2 * H], U8, "w3_raw")
+        for a in range(PASSES):
+            nc.sync.dma_start(out=w3_raw[:, 2 * H * a : 2 * H * (a + 1)].bitcast(I32), in_=w3_words[a].bitcast(I32))
+        b2_sb = held([P, PACK], F32, "b2_sb")
+        gain_sb = held([P, PACK], F32, "gain_sb")
+        nc.sync.dma_start(out=b2_sb[:], in_=b2.rearrange("(p t) -> p t", t=PACK))
+        nc.sync.dma_start(out=gain_sb[:], in_=gain.rearrange("(p t) -> p t", t=PACK))
+        nc.sync.dma_start(list2[:], offs2)
+        nc.sync.dma_start(list3[:], offs3)
+
+        def load_weight(w, a, name):
+            raw = held([P, PACK * H], F32, name)
+            nc.sync.dma_start(out=raw[:], in_=w[512 * a : 512 * (a + 1), :].rearrange("(p j) c -> p (j c)", j=PACK))
+            return raw
+
+        w2_raw = [load_weight(w2, 0, "w2_raw0")]
+        load_scale_rows(nc.sync, tab_plane, tab_scales)
+        w2_raw.append(load_weight(w2, 1, "w2_raw1"))
+        load_scale_rows(nc.sync, w3_plane_raw, w3_scales)
+        tab_sb = []
+        for a in range(PASSES):
+            words = held([P, T], U32, f"tab{a}")
+            nc.sync.dma_start(out=words[:].bitcast(I32), in_=tab_words[a].rearrange("p t i -> p (t i)").bitcast(I32))
+            tab_sb.append(words)
+        w1_raw = [load_weight(w1, a, f"w1_raw{a}") for a in range(PASSES)]
+        wgs_rows = wgs.rearrange("(q t) j -> q t j", t=PACK)
+        page_rows = page0.rearrange("(p t) c -> p t c", t=PACK)
+        wgs_sb, pages = [], []
+        for t in range(PACK):
+            dealt = held([P, S], F32, f"wgs{t}")
+            for q in range(4):
+                nc.sync.dma_start(out=dealt[32 * q : 32 * (q + 1), :], in_=wgs_rows[:, t, :])
+            wgs_sb.append(dealt)
+            page = held([P, T2], F32, f"page{t}")
+            nc.sync.dma_start(out=page[:], in_=page_rows[:, t, :])
+            pages.append(page)
+        wgt_sb = held([P, M], F32, "wgt_sb")
+        nc.sync.dma_start(out=wgt_sb[:], in_=wgt)
+        w4_sb = held([P, N], U32, "w4_sb")
+        nc.sync.dma_start(out=w4_sb[:].bitcast(I32), in_=w4_words[0].rearrange("p c i -> p (c i)").bitcast(I32))
+
+        load_scale_rows(nc.sync, w4_plane, w4_scales)
+
+        w3_sb = held([P, PASSES * 2 * H], U8, "w3_sb")
+        w3_plane = held([P, PASSES * H], U8, "w3_plane")
+        nc.vector.tensor_copy(
+            out=w3_sb[:].bitcast(U16).rearrange("p (a t m) -> p a m t", a=PASSES, t=PACK),
+            in_=w3_raw[:].bitcast(U16).rearrange("p (a m t) -> p a m t", a=PASSES, t=PACK),
+        )
+        turn_bias = held([P, PACK], F32, "turn_bias")
+        nc.vector.tensor_scalar(turn_bias[:], b2_sb[:], 1.0 / TWO_PI, 0.25, ALU.mult, ALU.add)
+
+        v_plane = []
+        for a in range(PASSES):
+            plane = held([P, S], U8, f"v_plane{a}")
+            nc.vector.tensor_copy(plane[:], tab_plane[:, a * T : (a + 1) * T].indirect(list1[:]))
+            v_plane.append(plane)
+
+        def round_weight(copy, raw, name, tag=""):
+            grouped = held([P, PACK * H], BF16, name, tag)
+            copy(
+                out=grouped[:].rearrange("p (t m j) -> p m t j", t=PACK, j=PACK),
+                in_=raw[:].rearrange("p (j m t) -> p m t j", j=PACK, t=PACK),
+            )
+            return grouped
+
+        def quantize(grouped, codes, plane):
+            nc.vector.quantize_mx(out=codes[:].bitcast(FP8X4), scales=plane[:], in_=grouped[:])
+
+        def quantize_weight(grouped, name):
+            codes = held([P, H], U32, name + "_codes")
+            plane = held([P, H], U8, name + "_plane")
+            quantize(grouped, codes, plane)
+            return codes, plane
+
+        w2_q = [quantize_weight(round_weight(nc.scalar.copy, w2_raw[a], f"w2_bf{a}"), f"w2_{a}") for a in range(PASSES)]
+
+        nc.vector.tensor_copy(
+            out=w3_plane[:].rearrange("p (a t m) -> p a m t", a=PASSES, t=PACK),
+            in_=w3_plane_raw[:].rearrange("p (a m t) -> p a m t", a=PASSES, t=PACK),
+        )
+        v_words = {}
+        for a, half in ((0, 0), (1, 0), (0, 1), (1, 1)):
+            words = held([P, HALF], U32, f"v{a}{half}")
+            nc.vector.tensor_copy(words[:], tab_sb[a][:].indirect(list1[:, 32 * half : 32 * (half + 1)]))
+            v_words[a, half] = words
+
+        def product(bank, stationary, half):
+            for a in range(PASSES):
+                codes, plane = stationary(a)
+                nc.tensor.matmul_mx(
+                    out=bank[:], lhsT=codes, lhsT_scale=plane,
+                    rhs=v_words[a, half][:].bitcast(FP8X4),
+                    rhs_scale=v_plane[a][:, HALF * half : HALF * (half + 1)],
+                    start=(a == 0), stop=(a == PASSES - 1),
+                )
+
+        def e4m3_slice(quantized, t):
+            return lambda a: (quantized[a][0][:, P * t : P * (t + 1)].bitcast(FP8X4), quantized[a][1][:, P * t : P * (t + 1)])
+
+        def w3_slice(t):
+            return lambda a: (
+                w3_sb[:, 2 * (H * a + P * t) : 2 * (H * a + P * (t + 1))].bitcast(FP4X4),
+                w3_plane[:, H * a + P * t : H * a + P * (t + 1)],
+            )
+
+        units = [(t, half) for t in range(PACK) for half in range(S // HALF)]
+
+        def cosine(unit):
+            t, half = unit
+            bank = psum.tile([P, HALF], F32, name="angle_bank", tag="angle", bufs=3)
+            product(bank, e4m3_slice(w2_q, t), half)
+            turns = ring.tile([P, HALF], F32, name="turns")
+            nc.scalar.activation(turns[:], bank[:], ACT.Identity, bias=turn_bias[:, t : t + 1], scale=1.0 / TWO_PI)
+            whole = ring.tile([P, HALF], U32, name="whole")
+            nc.scalar.activation(whole[:], turns[:], ACT.Copy, bias=ROUNDER, scale=1.0)
+            rest = ring.tile([P, HALF], F32, name="rest", bufs=2)
+            nc.vector.scalar_tensor_tensor(rest[:], whole[:].bitcast(I32), ROUNDER, turns[:], ALU.subtract, ALU.subtract)
+            lean = ring.tile([P, HALF], F32, name="lean")
+            nc.scalar.activation(lean[:], rest[:], ACT.Sin, scale=-TWO_PI)
+            return lean
+
+        AHEAD = 2
+        leans = [cosine(unit) for unit in units[:AHEAD]]
+        w1_q = [quantize_weight(round_weight(nc.vector.tensor_copy, w1_raw[a], f"w1_bf{a}", "w2_bf1"), f"w1_{a}") for a in range(PASSES)]
+
+        def join(i):
+            t, half = units[i]
+            slip_bank = psum.tile([P, HALF], F32, name="slip_bank", tag="slip", bufs=2)
+            product(slip_bank, e4m3_slice(w1_q, t), half)
+            load_bank = psum.tile([P, HALF], F32, name="load_bank", tag="load", bufs=3)
+            product(load_bank, w3_slice(t), half)
+            slip = ring.tile([P, HALF], F32, name="slip", bufs=2)
+            nc.scalar.activation(slip[:], slip_bank[:], ACT.Tanh)
+            joined = ring.tile([P, HALF], F32, name="joined", bufs=2)
+            nc.vector.scalar_tensor_tensor(joined[:], slip[:], gain_sb[:, t : t + 1], leans[i][:], ALU.mult, ALU.mult)
+            return joined, load_bank
+
+        def add_load(joined, load_bank):
+            cells = ring.tile([P, HALF], F32, name="cells", bufs=2)
+            nc.vector.tensor_tensor(cells[:], joined[:], load_bank[:], ALU.add)
+            return cells
+
+        joins = [join(0)]
+        news = [add_load(*joins[0])]
+        joins.append(join(1))
+        for i, (t, half) in enumerate(units):
+            cells = news[i]
+            if i + AHEAD < len(units):
+                leans.append(cosine(units[i + AHEAD]))
+            if i > 0 and i + 1 < len(units):
+                news.append(add_load(*joins[i + 1]))
+            nc.vector.tensor_tensor(
+                pages[t][:].indirect(list2[:, 32 * half : 32 * (half + 1)]),
+                cells[:], wgs_sb[t][:, HALF * half : HALF * (half + 1)], ALU.mult,
+            )
+            if i == 0:
+                news.append(add_load(*joins[1]))
+            if i + AHEAD < len(units):
+                joins.append(join(i + AHEAD))
+
+        first_two = held([P, PACK * (CHUNKS[0] + CHUNKS[1])], F32, "picked01", tag="wgs3")
+        out_rows = out.rearrange("(g p) m -> p g m", p=P)
+        groups = N // P
+        m0 = 0
+        for c, width in enumerate(CHUNKS):
+            if c < 2:
+                region = first_two[:, PACK * m0 : PACK * (m0 + width)]
+            else:
+                region = held([P, PACK * width], F32, f"picked{c}", tag=f"x_bf{c - 2}")[:]
+            for t in range(PACK):
+                nc.vector.tensor_tensor(
+                    region[:, width * t : width * (t + 1)],
+                    pages[t][:].indirect(list3[:, m0 // 16 : (m0 + width) // 16]),
+                    wgt_sb[:, m0 : m0 + width], ALU.mult,
+                )
+            x_bf = held([P, PACK * width], BF16, f"x_bf{c}")
+            weave = nc.vector.tensor_copy if c >= 3 else nc.scalar.copy
+            weave(out=x_bf[:].rearrange("p (m t) -> p m t", t=PACK), in_=region.rearrange("p (t m) -> p m t", t=PACK))
+            x_codes = held([P, width], U32, f"x_codes{c}")
+            x_plane = held([P, width], U8, f"x_plane{c}")
+            quantize(x_bf, x_codes, x_plane)
+            staged = held([P, groups * width], F32, f"staged{c}", tag=("w2_raw0", "w2_raw1", "w1_raw0", "w1_raw1", "tab0", "tab1")[c])
+            per_bank = 2 if width == 256 else 3
+            for b, (tag, bufs) in enumerate((("angle", 3), ("slip", 2), ("load", 3))[: groups // per_bank]):
+                bank = psum.tile([P, per_bank * width], F32, name="out_bank", tag=tag, bufs=bufs)
+                for i in range(per_bank):
+                    g = per_bank * b + i
+                    nc.tensor.matmul_mx(
+                        out=bank[:, width * i : width * (i + 1)],
+                        lhsT=w4_sb[:, P * g : P * (g + 1)].bitcast(FP8X4), lhsT_scale=w4_plane[:, P * g : P * (g + 1)],
+                        rhs=x_codes[:].bitcast(FP8X4), rhs_scale=x_plane[:], start=True, stop=True,
+                    )
+                empty = nc.vector.tensor_copy if (c >= 4 and b == 1) else nc.scalar.copy
+                empty(out=staged[:, per_bank * width * b : per_bank * width * (b + 1)], in_=bank[:])
+            nc.sync.dma_start(out=out_rows[:, :, m0 : m0 + width], in_=staged[:].rearrange("p (g m) -> p g m", g=groups))
+            m0 = m0 + width

@@ -23,7 +23,9 @@ PASSES = K // (P * PACK)
 HALF = 512
 TWO_PI = 2.0 * math.pi
 ROUNDER = 1.5 * 2.0**23
-CHUNKS = (128, 128, 256, 256, 128, 128)
+CHUNKS = (128, 256, 256, 256, 128)
+AHEAD = 1
+SCALAR_SHARE = 0
 
 
 def tile_list_lean_grip_features_kernel(
@@ -39,67 +41,85 @@ def tile_list_lean_grip_features_kernel(
         def held(shape, dtype, name, tag=""):
             return keep.tile(shape, dtype, name=name, tag=tag or name, align_bytes=64)
 
-        def load_scale_rows(queue, plane, scales):
+        def load_scale_rows(plane, scales):
             passes = scales.shape[0]
             for q in range(4):
-                queue.dma_start(
+                nc.sync.dma_start(
                     out=plane[32 * q : 32 * q + 4, :].bitcast(I32).rearrange("r (a c) -> r a c", a=passes),
                     in_=scales[:, 4 * q : 4 * q + 4, :].bitcast(I32).rearrange("a r c -> r a c"),
                 )
+
+        def load_weight(queue, w, a, name):
+            raw = held([P, PACK * H], F32, name)
+            queue.dma_start(out=raw[:], in_=w[512 * a : 512 * (a + 1), :].rearrange("(p j) c -> p (j c)", j=PACK))
+            return raw
 
         list1 = keep.tile([P, S // 16], U16, name="list1")
         list2 = keep.tile([P, S // 16], U16, name="list2")
         list3 = keep.tile([P, M // 16], U16, name="list3")
 
-        tab_plane = held([P, PASSES * T], U8, "tab_plane")
+        tab_plane = held([P, T], U8, "tab_plane")
         w3_plane_raw = held([P, PASSES * H], U8, "w3_plane_raw")
+        v_plane_low = held([P, S], U8, "v_plane_low")
         w4_plane = held([P, N], U8, "w4_plane")
-        for plane in (tab_plane, w3_plane_raw, w4_plane):
-            nc.vector.memset(plane[:].bitcast(I32), 0)
+        for plane in (tab_plane, w3_plane_raw, v_plane_low, w4_plane):
+            nc.gpsimd.memset(plane[:].bitcast(I32), 0)
 
+        w2_raw = [load_weight(nc.scalar, w2, 0, "w2_raw0")]
+        warm = held([P, 2], F32, "warm")
+        nc.vector.memset(warm[:, 0:1], 0.0)
+        nc.scalar.activation(warm[:, 1:2], warm[:, 0:1], ACT.Silu)
         nc.sync.dma_start(list1[:], offs)
+        for q in range(4):
+            nc.sync.dma_start(out=tab_plane[32 * q : 32 * q + 8, :].bitcast(I32), in_=tab_scales[:, 4 * q : 4 * q + 4, :].bitcast(I32))
         w3_raw = held([P, PASSES * 2 * H], U8, "w3_raw")
-        for a in range(PASSES):
-            nc.sync.dma_start(out=w3_raw[:, 2 * H * a : 2 * H * (a + 1)].bitcast(I32), in_=w3_words[a].bitcast(I32))
+        nc.sync.dma_start(
+            out=w3_raw[:].bitcast(I32).rearrange("p (a c) -> p a c", a=PASSES),
+            in_=w3_words.bitcast(I32).rearrange("a p c -> p a c"),
+        )
+        tab_sb = []
+        def load_tab(a):
+            words = held([P, T], U32, f"tab{a}")
+            nc.sync.dma_start(out=words[:].bitcast(I32), in_=tab_words[a].rearrange("p t i -> p (t i)").bitcast(I32))
+            tab_sb.append(words)
+        load_tab(0)
         b2_sb = held([P, PACK], F32, "b2_sb")
         gain_sb = held([P, PACK], F32, "gain_sb")
         nc.sync.dma_start(out=b2_sb[:], in_=b2.rearrange("(p t) -> p t", t=PACK))
         nc.sync.dma_start(out=gain_sb[:], in_=gain.rearrange("(p t) -> p t", t=PACK))
+        load_scale_rows(w3_plane_raw, w3_scales)
+        load_tab(1)
         nc.sync.dma_start(list2[:], offs2)
-        nc.sync.dma_start(list3[:], offs3)
-
-        def load_weight(w, a, name):
-            raw = held([P, PACK * H], F32, name)
-            nc.sync.dma_start(out=raw[:], in_=w[512 * a : 512 * (a + 1), :].rearrange("(p j) c -> p (j c)", j=PACK))
-            return raw
-
-        w2_raw = [load_weight(w2, 0, "w2_raw0")]
-        load_scale_rows(nc.sync, tab_plane, tab_scales)
-        w2_raw.append(load_weight(w2, 1, "w2_raw1"))
-        load_scale_rows(nc.sync, w3_plane_raw, w3_scales)
-        tab_sb = []
-        for a in range(PASSES):
-            words = held([P, T], U32, f"tab{a}")
-            nc.sync.dma_start(out=words[:].bitcast(I32), in_=tab_words[a].rearrange("p t i -> p (t i)").bitcast(I32))
-            tab_sb.append(words)
-        w1_raw = [load_weight(w1, a, f"w1_raw{a}") for a in range(PASSES)]
+        v_plane = held([P, S], U8, "v_plane")
+        nc.vector.tensor_copy(v_plane[:], tab_plane[:].indirect(list1[:]))
+        for q in range(4):
+            nc.sync.dma_start(out=v_plane_low[32 * q : 32 * q + 4, :].bitcast(I32), in_=v_plane[32 * q + 4 : 32 * q + 8, :].bitcast(I32))
+        w2_raw.append(load_weight(nc.sync, w2, 1, "w2_raw1"))
+        w1_raw = [load_weight(nc.sync, w1, a, f"w1_raw{a}") for a in range(PASSES)]
         wgs_rows = wgs.rearrange("(q t) j -> q t j", t=PACK)
         page_rows = page0.rearrange("(p t) c -> p t c", t=PACK)
-        wgs_sb, pages = [], []
-        for t in range(PACK):
-            dealt = held([P, S], F32, f"wgs{t}")
+        wgs_sb = [held([P, S + HALF], F32, f"wgs{t}") for t in range(PACK)]
+        pages = [held([P, T2], F32, f"page{t}") for t in range(PACK)]
+
+        def load_wgs(t, cols):
             for q in range(4):
-                nc.sync.dma_start(out=dealt[32 * q : 32 * (q + 1), :], in_=wgs_rows[:, t, :])
-            wgs_sb.append(dealt)
-            page = held([P, T2], F32, f"page{t}")
-            nc.sync.dma_start(out=page[:], in_=page_rows[:, t, :])
-            pages.append(page)
+                nc.sync.dma_start(out=wgs_sb[t][32 * q : 32 * (q + 1), cols], in_=wgs_rows[:, t, cols])
+
+        load_wgs(0, slice(0, HALF))
+        nc.sync.dma_start(out=pages[0][:], in_=page_rows[:, 0, :])
+        load_wgs(0, slice(HALF, S))
+        for t in range(1, PACK - 1):
+            load_wgs(t, slice(0, S))
+            nc.sync.dma_start(out=pages[t][:], in_=page_rows[:, t, :])
+        nc.sync.dma_start(list3[:], offs3)
         wgt_sb = held([P, M], F32, "wgt_sb")
         nc.sync.dma_start(out=wgt_sb[:], in_=wgt)
         w4_sb = held([P, N], U32, "w4_sb")
         nc.sync.dma_start(out=w4_sb[:].bitcast(I32), in_=w4_words[0].rearrange("p c i -> p (c i)").bitcast(I32))
+        load_scale_rows(w4_plane, w4_scales)
+        load_wgs(PACK - 1, slice(0, S))
+        nc.sync.dma_start(out=pages[PACK - 1][:], in_=page_rows[:, PACK - 1, :])
 
-        load_scale_rows(nc.sync, w4_plane, w4_scales)
 
         w3_sb = held([P, PASSES * 2 * H], U8, "w3_sb")
         w3_plane = held([P, PASSES * H], U8, "w3_plane")
@@ -107,53 +127,61 @@ def tile_list_lean_grip_features_kernel(
             out=w3_sb[:].bitcast(U16).rearrange("p (a t m) -> p a m t", a=PASSES, t=PACK),
             in_=w3_raw[:].bitcast(U16).rearrange("p (a m t) -> p a m t", a=PASSES, t=PACK),
         )
+        nc.vector.tensor_copy(
+            out=w3_plane[:].rearrange("p (a t m) -> p a m t", a=PASSES, t=PACK),
+            in_=w3_plane_raw[:].rearrange("p (a m t) -> p a m t", a=PASSES, t=PACK),
+        )
         turn_bias = held([P, PACK], F32, "turn_bias")
         nc.vector.tensor_scalar(turn_bias[:], b2_sb[:], 1.0 / TWO_PI, 0.25, ALU.mult, ALU.add)
-
-        v_plane = []
-        for a in range(PASSES):
-            plane = held([P, S], U8, f"v_plane{a}")
-            nc.vector.tensor_copy(plane[:], tab_plane[:, a * T : (a + 1) * T].indirect(list1[:]))
-            v_plane.append(plane)
-
-        def round_weight(copy, raw, name, tag=""):
-            grouped = held([P, PACK * H], BF16, name, tag)
-            copy(
-                out=grouped[:].rearrange("p (t m j) -> p m t j", t=PACK, j=PACK),
-                in_=raw[:].rearrange("p (j m t) -> p m t j", j=PACK, t=PACK),
-            )
-            return grouped
 
         def quantize(grouped, codes, plane):
             nc.vector.quantize_mx(out=codes[:].bitcast(FP8X4), scales=plane[:], in_=grouped[:])
 
-        def quantize_weight(grouped, name):
+        def quantize_weight(raw, name, scalar_share):
+            grouped = held([P, PACK * H], BF16, name + "_bf")
+            dst = grouped[:].rearrange("p (t m j) -> p m t j", t=PACK, j=PACK)
+            src = raw[:].rearrange("p (j m t) -> p m t j", j=PACK, t=PACK)
+            if scalar_share > 0:
+                nc.scalar.copy(out=dst[:, :scalar_share], in_=src[:, :scalar_share])
+            if scalar_share < P:
+                nc.vector.tensor_copy(out=dst[:, scalar_share:], in_=src[:, scalar_share:])
             codes = held([P, H], U32, name + "_codes")
             plane = held([P, H], U8, name + "_plane")
             quantize(grouped, codes, plane)
             return codes, plane
 
-        w2_q = [quantize_weight(round_weight(nc.scalar.copy, w2_raw[a], f"w2_bf{a}"), f"w2_{a}") for a in range(PASSES)]
+        def quantize_by_slice(raw, name):
+            grouped = held([P, PACK * H], BF16, name + "_bf")
+            dst = grouped[:].rearrange("p (t m j) -> p m t j", t=PACK, j=PACK)
+            src = raw[:].rearrange("p (j m t) -> p m t j", j=PACK, t=PACK)
+            codes = held([P, H], U32, name + "_codes")
+            plane = held([P, H], U8, name + "_plane")
+            for lo, hi in ((0, 1), (1, PACK)):
+                nc.vector.tensor_copy(out=dst[:, :, lo:hi], in_=src[:, :, lo:hi])
+                quantize(grouped[:, H * lo : H * hi], codes[:, P * lo : P * hi], plane[:, P * lo : P * hi])
+            return codes, plane
 
-        nc.vector.tensor_copy(
-            out=w3_plane[:].rearrange("p (a t m) -> p a m t", a=PASSES, t=PACK),
-            in_=w3_plane_raw[:].rearrange("p (a m t) -> p a m t", a=PASSES, t=PACK),
-        )
+        w2_q = [quantize_weight(w2_raw[0], "w2_0", P), quantize_weight(w2_raw[1], "w2_1", 96)]
+
         v_words = {}
-        for a, half in ((0, 0), (1, 0), (0, 1), (1, 1)):
-            words = held([P, HALF], U32, f"v{a}{half}")
-            nc.vector.tensor_copy(words[:], tab_sb[a][:].indirect(list1[:, 32 * half : 32 * (half + 1)]))
-            v_words[a, half] = words
+        for half in range(S // HALF):
+            for a in range(PASSES):
+                words = held([P, HALF], U32, f"v{a}{half}")
+                nc.vector.tensor_copy(words[:], tab_sb[a][:].indirect(list1[:, 32 * half : 32 * (half + 1)]))
+                v_words[a, half] = words
 
-        def product(bank, stationary, half):
+        def product(bank, stationary, planes, half):
             for a in range(PASSES):
                 codes, plane = stationary(a)
                 nc.tensor.matmul_mx(
                     out=bank[:], lhsT=codes, lhsT_scale=plane,
                     rhs=v_words[a, half][:].bitcast(FP8X4),
-                    rhs_scale=v_plane[a][:, HALF * half : HALF * (half + 1)],
+                    rhs_scale=planes[a][:, HALF * half : HALF * (half + 1)],
                     start=(a == 0), stop=(a == PASSES - 1),
                 )
+
+        packed_planes = (v_plane[:], v_plane[4:, :])
+        low_planes = (v_plane[:], v_plane_low[:])
 
         def e4m3_slice(quantized, t):
             return lambda a: (quantized[a][0][:, P * t : P * (t + 1)].bitcast(FP8X4), quantized[a][1][:, P * t : P * (t + 1)])
@@ -164,86 +192,97 @@ def tile_list_lean_grip_features_kernel(
                 w3_plane[:, H * a + P * t : H * a + P * (t + 1)],
             )
 
+        def rotation(pool, dtype, name, count):
+            return [pool.tile([P, HALF], dtype, name=f"{name}{i}", tag=f"{name}{i}", bufs=1) for i in range(count)]
+
+        pair_banks = rotation(psum, F32, "pair_bank", 4)
+        load_banks = rotation(psum, F32, "load_bank", 3)
+        out_banks = rotation(psum, F32, "out_bank", 1) + pair_banks + load_banks
+        turns_ring = rotation(ring, F32, "turns", 3)
+        whole_ring = rotation(ring, U32, "whole", 3)
+        rest_ring = rotation(ring, F32, "rest", 4)
+        lean_ring = rotation(ring, F32, "lean", 3)
+        slip_ring = rotation(ring, F32, "slip", 2)
+        joined_ring = rotation(ring, F32, "joined", 2)
+        cells_ring = rotation(ring, F32, "cells", 3)
         units = [(t, half) for t in range(PACK) for half in range(S // HALF)]
 
-        def cosine(unit):
-            t, half = unit
-            bank = psum.tile([P, HALF], F32, name="angle_bank", tag="angle", bufs=3)
-            product(bank, e4m3_slice(w2_q, t), half)
-            turns = ring.tile([P, HALF], F32, name="turns")
+        def cosine(i):
+            t, half = units[i]
+            bank = pair_banks[i % len(pair_banks)]
+            product(bank, e4m3_slice(w2_q, t), packed_planes, half)
+            turns = turns_ring[i % len(turns_ring)]
             nc.scalar.activation(turns[:], bank[:], ACT.Identity, bias=turn_bias[:, t : t + 1], scale=1.0 / TWO_PI)
-            whole = ring.tile([P, HALF], U32, name="whole")
+            whole = whole_ring[i % len(whole_ring)]
             nc.scalar.activation(whole[:], turns[:], ACT.Copy, bias=ROUNDER, scale=1.0)
-            rest = ring.tile([P, HALF], F32, name="rest", bufs=2)
+            rest = rest_ring[i % len(rest_ring)]
             nc.vector.scalar_tensor_tensor(rest[:], whole[:].bitcast(I32), ROUNDER, turns[:], ALU.subtract, ALU.subtract)
-            lean = ring.tile([P, HALF], F32, name="lean")
-            nc.scalar.activation(lean[:], rest[:], ACT.Sin, scale=-TWO_PI)
-            return lean
+            return rest
 
-        AHEAD = 2
-        leans = [cosine(unit) for unit in units[:AHEAD]]
-        w1_q = [quantize_weight(round_weight(nc.vector.tensor_copy, w1_raw[a], f"w1_bf{a}", "w2_bf1"), f"w1_{a}") for a in range(PASSES)]
+        leans = [cosine(i) for i in range(1)]
+        w1_q = [quantize_weight(w1_raw[0], "w1_0", 0), quantize_by_slice(w1_raw[1], "w1_1")]
 
         def join(i):
             t, half = units[i]
-            slip_bank = psum.tile([P, HALF], F32, name="slip_bank", tag="slip", bufs=2)
-            product(slip_bank, e4m3_slice(w1_q, t), half)
-            load_bank = psum.tile([P, HALF], F32, name="load_bank", tag="load", bufs=3)
-            product(load_bank, w3_slice(t), half)
-            slip = ring.tile([P, HALF], F32, name="slip", bufs=2)
+            slip_bank = pair_banks[i % len(pair_banks)]
+            product(slip_bank, e4m3_slice(w1_q, t), packed_planes, half)
+            load_bank = load_banks[i % len(load_banks)]
+            product(load_bank, w3_slice(t), low_planes, half)
+            lean = lean_ring[i % len(lean_ring)]
+            nc.scalar.activation(lean[:], leans[i][:], ACT.Sin, scale=-TWO_PI)
+            slip = slip_ring[i % len(slip_ring)]
             nc.scalar.activation(slip[:], slip_bank[:], ACT.Tanh)
-            joined = ring.tile([P, HALF], F32, name="joined", bufs=2)
-            nc.vector.scalar_tensor_tensor(joined[:], slip[:], gain_sb[:, t : t + 1], leans[i][:], ALU.mult, ALU.mult)
+            joined = joined_ring[i % len(joined_ring)]
+            nc.vector.scalar_tensor_tensor(joined[:], slip[:], gain_sb[:, t : t + 1], lean[:], ALU.mult, ALU.mult)
             return joined, load_bank
 
-        def add_load(joined, load_bank):
-            cells = ring.tile([P, HALF], F32, name="cells", bufs=2)
+        def add_load(i, joined, load_bank):
+            cells = cells_ring[i % len(cells_ring)]
             nc.vector.tensor_tensor(cells[:], joined[:], load_bank[:], ALU.add)
             return cells
 
-        joins = [join(0)]
-        news = [add_load(*joins[0])]
-        joins.append(join(1))
-        for i, (t, half) in enumerate(units):
-            cells = news[i]
-            if i + AHEAD < len(units):
-                leans.append(cosine(units[i + AHEAD]))
-            if i > 0 and i + 1 < len(units):
-                news.append(add_load(*joins[i + 1]))
+        def scatter(i, cells):
+            t, half = units[i]
             nc.vector.tensor_tensor(
                 pages[t][:].indirect(list2[:, 32 * half : 32 * (half + 1)]),
                 cells[:], wgs_sb[t][:, HALF * half : HALF * (half + 1)], ALU.mult,
             )
-            if i == 0:
-                news.append(add_load(*joins[1]))
-            if i + AHEAD < len(units):
-                joins.append(join(i + AHEAD))
 
-        first_two = held([P, PACK * (CHUNKS[0] + CHUNKS[1])], F32, "picked01", tag="wgs3")
+        for i in range(len(units)):
+            joined = join(i)
+            if i == 0:
+                leans.extend(cosine(ahead) for ahead in range(len(leans), len(pair_banks)))
+            scatter(i, add_load(i, *joined))
+            if i + len(pair_banks) < len(units):
+                leans.append(cosine(i + len(pair_banks)))
+
+        stages = (wgs_sb[PACK - 1], wgs_sb[PACK - 2])
         out_rows = out.rearrange("(g p) m -> p g m", p=P)
         groups = N // P
-        m0 = 0
-        for c, width in enumerate(CHUNKS):
-            if c < 2:
-                region = first_two[:, PACK * m0 : PACK * (m0 + width)]
-            else:
-                region = held([P, PACK * width], F32, f"picked{c}", tag=f"x_bf{c - 2}")[:]
+        starts = [sum(CHUNKS[:c]) for c in range(len(CHUNKS))]
+        last = len(CHUNKS) - 1
+
+        def pick(c):
+            width, m0 = CHUNKS[c], starts[c]
+            picked = stages[c % 2][:, : PACK * width]
             for t in range(PACK):
                 nc.vector.tensor_tensor(
-                    region[:, width * t : width * (t + 1)],
+                    picked[:, width * t : width * (t + 1)],
                     pages[t][:].indirect(list3[:, m0 // 16 : (m0 + width) // 16]),
                     wgt_sb[:, m0 : m0 + width], ALU.mult,
                 )
-            x_bf = held([P, PACK * width], BF16, f"x_bf{c}")
+            first_word = 3 * CHUNKS[min(c + 1, last)]
+            x_bf = stages[(c + 1) % 2][:, first_word : first_word + 2 * width].bitcast(BF16)
             weave = nc.vector.tensor_copy if c >= 3 else nc.scalar.copy
-            weave(out=x_bf[:].rearrange("p (m t) -> p m t", t=PACK), in_=region.rearrange("p (t m) -> p m t", t=PACK))
-            x_codes = held([P, width], U32, f"x_codes{c}")
-            x_plane = held([P, width], U8, f"x_plane{c}")
-            quantize(x_bf, x_codes, x_plane)
-            staged = held([P, groups * width], F32, f"staged{c}", tag=("w2_raw0", "w2_raw1", "w1_raw0", "w1_raw1", "tab0", "tab1")[c])
+            weave(out=x_bf.rearrange("p (m t) -> p m t", t=PACK), in_=picked.rearrange("p (t m) -> p m t", t=PACK))
+            return x_bf
+
+        def features(c, x_codes, x_plane, used):
+            width, m0 = CHUNKS[c], starts[c]
             per_bank = 2 if width == 256 else 3
-            for b, (tag, bufs) in enumerate((("angle", 3), ("slip", 2), ("load", 3))[: groups // per_bank]):
-                bank = psum.tile([P, per_bank * width], F32, name="out_bank", tag=tag, bufs=bufs)
+            staged = held([P, groups * width], F32, f"staged{c}", tag=("w2_raw0", "w2_raw1", "tab0", "tab1", "w2_0_bf", "w2_1_bf")[c])
+            for b in range(groups // per_bank):
+                bank = out_banks[(used + b) % len(out_banks)][:, : per_bank * width]
                 for i in range(per_bank):
                     g = per_bank * b + i
                     nc.tensor.matmul_mx(
@@ -251,7 +290,19 @@ def tile_list_lean_grip_features_kernel(
                         lhsT=w4_sb[:, P * g : P * (g + 1)].bitcast(FP8X4), lhsT_scale=w4_plane[:, P * g : P * (g + 1)],
                         rhs=x_codes[:].bitcast(FP8X4), rhs_scale=x_plane[:], start=True, stop=True,
                     )
+                part = staged[:, per_bank * width * b : per_bank * width * (b + 1)]
                 empty = nc.vector.tensor_copy if (c >= 4 and b == 1) else nc.scalar.copy
-                empty(out=staged[:, per_bank * width * b : per_bank * width * (b + 1)], in_=bank[:])
-            nc.sync.dma_start(out=out_rows[:, :, m0 : m0 + width], in_=staged[:].rearrange("p (g m) -> p g m", g=groups))
-            m0 = m0 + width
+                empty(out=part, in_=bank)
+                nc.sync.dma_start(
+                    out=out_rows[:, per_bank * b : per_bank * (b + 1), m0 : m0 + width],
+                    in_=part.rearrange("p (g m) -> p g m", g=per_bank),
+                )
+
+        waiting = None
+        for c, width in enumerate(CHUNKS):
+            x_bf = pick(c)
+            if waiting is not None:
+                features(c - 1, *waiting, 3 * (c - 1))
+            waiting = (held([P, width], U32, f"x_codes{c}"), held([P, width], U8, f"x_plane{c}"))
+            quantize(x_bf, *waiting)
+        features(last, *waiting, 3 * last)

@@ -98,7 +98,7 @@ def tile_list_lean_grip_features_kernel(
         w1_raw = [load_weight(nc.sync, w1, a, f"w1_raw{a}") for a in range(PASSES)]
         wgs_rows = wgs.rearrange("(q t) j -> q t j", t=PACK)
         page_rows = page0.rearrange("(p t) c -> p t c", t=PACK)
-        wgs_sb = [held([P, S + HALF], F32, f"wgs{t}") for t in range(PACK)]
+        wgs_sb = [held([P, S], F32, f"wgs{t}") for t in range(PACK)]
         pages = [held([P, T2], F32, f"page{t}") for t in range(PACK)]
 
         def load_wgs(t, cols):
@@ -202,9 +202,11 @@ def tile_list_lean_grip_features_kernel(
         whole_ring = rotation(ring, U32, "whole", 3)
         rest_ring = rotation(ring, F32, "rest", 4)
         lean_ring = rotation(ring, F32, "lean", 3)
-        slip_ring = rotation(ring, F32, "slip", 2)
-        joined_ring = rotation(ring, F32, "joined", 2)
-        cells_ring = rotation(ring, F32, "cells", 3)
+        wide = [held([P, S + HALF], F32, f"slip{i}") for i in range(4)]
+        slip_ring = [tile[:, :HALF] for tile in wide]
+        joined_ring = rotation(ring, F32, "joined", 3)
+        count_ring = rotation(ring, F32, "count", 2)
+        first_weighted = held([P, HALF], F32, "first_weighted")
         units = [(t, half) for t in range(PACK) for half in range(S // HALF)]
 
         def cosine(i):
@@ -216,7 +218,12 @@ def tile_list_lean_grip_features_kernel(
             whole = whole_ring[i % len(whole_ring)]
             nc.scalar.activation(whole[:], turns[:], ACT.Copy, bias=ROUNDER, scale=1.0)
             rest = rest_ring[i % len(rest_ring)]
-            nc.vector.scalar_tensor_tensor(rest[:], whole[:].bitcast(I32), ROUNDER, turns[:], ALU.subtract, ALU.subtract)
+            if i < 4:
+                nc.vector.scalar_tensor_tensor(rest[:], whole[:].bitcast(I32), ROUNDER, turns[:], ALU.subtract, ALU.subtract)
+            else:
+                count = count_ring[i % len(count_ring)]
+                nc.scalar.activation(count[:], whole[:], ACT.Copy, bias=-ROUNDER, scale=1.0)
+                nc.gpsimd.tensor_tensor(rest[:], count[:], turns[:], ALU.subtract)
             return rest
 
         leans = [cosine(i) for i in range(1)]
@@ -233,30 +240,35 @@ def tile_list_lean_grip_features_kernel(
             slip = slip_ring[i % len(slip_ring)]
             nc.scalar.activation(slip[:], slip_bank[:], ACT.Tanh)
             joined = joined_ring[i % len(joined_ring)]
-            nc.vector.scalar_tensor_tensor(joined[:], slip[:], gain_sb[:, t : t + 1], lean[:], ALU.mult, ALU.mult)
+            (nc.vector if i < 1 else nc.gpsimd).tensor_tensor(joined[:], slip[:], lean[:], ALU.mult)
             return joined, load_bank
 
         def add_load(i, joined, load_bank):
-            cells = cells_ring[i % len(cells_ring)]
-            nc.vector.tensor_tensor(cells[:], joined[:], load_bank[:], ALU.add)
+            cells = rest_ring[i % len(rest_ring)]
+            t = units[i][0]
+            nc.vector.scalar_tensor_tensor(cells[:], joined[:], gain_sb[:, t : t + 1], load_bank[:], ALU.mult, ALU.add)
             return cells
 
         def scatter(i, cells):
             t, half = units[i]
-            nc.vector.tensor_tensor(
-                pages[t][:].indirect(list2[:, 32 * half : 32 * (half + 1)]),
-                cells[:], wgs_sb[t][:, HALF * half : HALF * (half + 1)], ALU.mult,
-            )
+            weighted = slip_ring[(i + 1) % len(slip_ring)] if i > 0 else first_weighted
+            (nc.vector if i < 1 else nc.gpsimd).tensor_tensor(weighted[:], cells[:], wgs_sb[t][:, HALF * half : HALF * (half + 1)], ALU.mult)
+            nc.vector.tensor_copy(pages[t][:].indirect(list2[:, 32 * half : 32 * (half + 1)]), weighted[:])
 
-        for i in range(len(units)):
-            joined = join(i)
-            if i == 0:
-                leans.extend(cosine(ahead) for ahead in range(len(leans), len(pair_banks)))
-            scatter(i, add_load(i, *joined))
-            if i + len(pair_banks) < len(units):
-                leans.append(cosine(i + len(pair_banks)))
+        ahead = len(pair_banks)
+        cells = [add_load(0, *join(0))]
+        leans.extend(cosine(i) for i in range(1, ahead))
+        scatter(0, cells[0])
+        leans.append(cosine(ahead))
+        cells.append(add_load(1, *join(1)))
+        for i in range(1, len(units)):
+            if i + 1 < len(units):
+                cells.append(add_load(i + 1, *join(i + 1)))
+            scatter(i, cells[i])
+            if i + ahead < len(units):
+                leans.append(cosine(i + ahead))
 
-        stages = (wgs_sb[PACK - 1], wgs_sb[PACK - 2])
+        stages = (wide[len(units) % len(wide)], wide[(len(units) - 1) % len(wide)])
         out_rows = out.rearrange("(g p) m -> p g m", p=P)
         groups = N // P
         starts = [sum(CHUNKS[:c]) for c in range(len(CHUNKS))]

@@ -23,7 +23,7 @@ PASSES = K // (P * PACK)
 HALF = 512
 TWO_PI = 2.0 * math.pi
 ROUNDER = 1.5 * 2.0**23
-CHUNKS = (128, 256, 256, 256, 128)
+CHUNKS = (256, 256, 256, 256)
 AHEAD = 1
 SCALAR_SHARE = 0
 
@@ -109,7 +109,7 @@ def tile_list_lean_grip_features_kernel(
         nc.sync.dma_start(out=pages[0][:], in_=page_rows[:, 0, :])
         load_wgs(0, slice(HALF, S))
         for t in range(1, PACK - 1):
-            load_wgs(t, slice(0, S))
+            nc.sync.dma_start(out=wgs_sb[t][:], in_=wgs_rows[:, t, :].unsqueeze(0).to_broadcast([4, 32, S]))
             nc.sync.dma_start(out=pages[t][:], in_=page_rows[:, t, :])
         nc.sync.dma_start(list3[:], offs3)
         wgt_sb = held([P, M], F32, "wgt_sb")
@@ -117,7 +117,7 @@ def tile_list_lean_grip_features_kernel(
         w4_sb = held([P, N], U32, "w4_sb")
         nc.sync.dma_start(out=w4_sb[:].bitcast(I32), in_=w4_words[0].rearrange("p c i -> p (c i)").bitcast(I32))
         load_scale_rows(w4_plane, w4_scales)
-        load_wgs(PACK - 1, slice(0, S))
+        nc.sync.dma_start(out=wgs_sb[PACK - 1][:], in_=wgs_rows[:, PACK - 1, :].unsqueeze(0).to_broadcast([4, 32, S]))
         nc.sync.dma_start(out=pages[PACK - 1][:], in_=page_rows[:, PACK - 1, :])
 
 
@@ -161,7 +161,7 @@ def tile_list_lean_grip_features_kernel(
                 quantize(grouped[:, H * lo : H * hi], codes[:, P * lo : P * hi], plane[:, P * lo : P * hi])
             return codes, plane
 
-        w2_q = [quantize_weight(w2_raw[0], "w2_0", P), quantize_weight(w2_raw[1], "w2_1", 96)]
+        w2_q = [quantize_weight(w2_raw[0], "w2_0", P), quantize_weight(w2_raw[1], "w2_1", 64)]
 
         v_words = {}
         for half in range(S // HALF):
@@ -217,8 +217,8 @@ def tile_list_lean_grip_features_kernel(
             nc.scalar.activation(turns[:], bank[:], ACT.Identity, bias=turn_bias[:, t : t + 1], scale=1.0 / TWO_PI)
             whole = whole_ring[i % len(whole_ring)]
             nc.scalar.activation(whole[:], turns[:], ACT.Copy, bias=ROUNDER, scale=1.0)
-            rest = rest_ring[i % len(rest_ring)]
-            if i < 4:
+            rest = rest_ring[(i if i < len(rest_ring) else i + 1) % len(rest_ring)]
+            if i < 3:
                 nc.vector.scalar_tensor_tensor(rest[:], whole[:].bitcast(I32), ROUNDER, turns[:], ALU.subtract, ALU.subtract)
             else:
                 count = count_ring[i % len(count_ring)]
@@ -227,7 +227,7 @@ def tile_list_lean_grip_features_kernel(
             return rest
 
         leans = [cosine(i) for i in range(1)]
-        w1_q = [quantize_weight(w1_raw[0], "w1_0", 0), quantize_by_slice(w1_raw[1], "w1_1")]
+        w1_q = [quantize_weight(w1_raw[0], "w1_0", 48), quantize_by_slice(w1_raw[1], "w1_1")]
 
         def join(i):
             t, half = units[i]
@@ -252,21 +252,20 @@ def tile_list_lean_grip_features_kernel(
         def scatter(i, cells):
             t, half = units[i]
             weighted = slip_ring[(i + 1) % len(slip_ring)] if i > 0 else first_weighted
-            (nc.vector if i < 1 else nc.gpsimd).tensor_tensor(weighted[:], cells[:], wgs_sb[t][:, HALF * half : HALF * (half + 1)], ALU.mult)
+            (nc.vector if i < 2 else nc.gpsimd).tensor_tensor(weighted[:], cells[:], wgs_sb[t][:, HALF * half : HALF * (half + 1)], ALU.mult)
             nc.vector.tensor_copy(pages[t][:].indirect(list2[:, 32 * half : 32 * (half + 1)]), weighted[:])
 
         ahead = len(pair_banks)
         cells = [add_load(0, *join(0))]
         leans.extend(cosine(i) for i in range(1, ahead))
         scatter(0, cells[0])
-        leans.append(cosine(ahead))
         cells.append(add_load(1, *join(1)))
         for i in range(1, len(units)):
             if i + 1 < len(units):
                 cells.append(add_load(i + 1, *join(i + 1)))
             scatter(i, cells[i])
-            if i + ahead < len(units):
-                leans.append(cosine(i + ahead))
+            if i + ahead - 1 < len(units):
+                leans.append(cosine(i + ahead - 1))
 
         stages = (wide[len(units) % len(wide)], wide[(len(units) - 1) % len(wide)])
         out_rows = out.rearrange("(g p) m -> p g m", p=P)
@@ -286,7 +285,7 @@ def tile_list_lean_grip_features_kernel(
             first_word = 3 * CHUNKS[min(c + 1, last)]
             x_bf = stages[(c + 1) % 2][:, first_word : first_word + 2 * width].bitcast(BF16)
             weave = nc.vector.tensor_copy if c >= 3 else nc.scalar.copy
-            weave(out=x_bf.rearrange("p (m t) -> p m t", t=PACK), in_=picked.rearrange("p (t m) -> p m t", t=PACK))
+            weave(out=x_bf.rearrange("p (c i t) -> p c t i", i=4, t=PACK), in_=picked.rearrange("p (t c i) -> p c t i", i=4, t=PACK))
             return x_bf
 
         def features(c, x_codes, x_plane, used):
@@ -303,7 +302,7 @@ def tile_list_lean_grip_features_kernel(
                         rhs=x_codes[:].bitcast(FP8X4), rhs_scale=x_plane[:], start=True, stop=True,
                     )
                 part = staged[:, per_bank * width * b : per_bank * width * (b + 1)]
-                empty = nc.vector.tensor_copy if (c >= 4 and b == 1) else nc.scalar.copy
+                empty = nc.vector.tensor_copy if (c >= 3 and b == 1) else nc.scalar.copy
                 empty(out=part, in_=bank)
                 nc.sync.dma_start(
                     out=out_rows[:, per_bank * b : per_bank * (b + 1), m0 : m0 + width],

import math
from contextlib import ExitStack

import concourse.mybir as mybir

K, T, S, H, T2, M, N = 1024, 2048, 1024, 512, 2048, 1024, 768
FLOPS = 2 * (3 * K * H * S + H * N * M)

F32 = mybir.dt.float32
BF16 = mybir.dt.bfloat16
I32 = mybir.dt.int32
U32 = mybir.dt.uint32
U16 = mybir.dt.uint16
U8 = mybir.dt.uint8
FP8X4 = mybir.dt.float8_e4m3fn_x4
FP4X4 = mybir.dt.float4_e2m1fn_x4
ACT = mybir.ActivationFunctionType
ALU = mybir.AluOpType

P = 128
PACK = 4
PASSES = K // (P * PACK)
HALF = 512
TWO_PI = 2.0 * math.pi
ROUNDER = 1.5 * 2.0**23
CHUNKS = (256, 256, 256, 256)
AHEAD = 1
SCALAR_SHARE = 0


def tile_list_lean_grip_features_kernel(
    tc, tab_words, tab_scales, offs, offs2, offs3, w1, w2, b2, gain, w3_words, w3_scales,
    page0, wgs, wgt, w4_words, w4_scales, out,
):
    nc = tc.nc
    with ExitStack() as ctx:
        keep = ctx.enter_context(tc.tile_pool(name="keep", bufs=1))
        ring = ctx.enter_context(tc.tile_pool(name="ring", bufs=3))
        psum = ctx.enter_context(tc.psum_pool(name="psum", bufs=1))

        def held(shape, dtype, name, tag=""):
            return keep.tile(shape, dtype, name=name, tag=tag or name, align_bytes=64)

        def load_scale_rows(plane, scales):
            passes = scales.shape[0]
            for q in range(4):
                nc.sync.dma_start(
                    out=plane[32 * q : 32 * q + 4, :].bitcast(I32).rearrange("r (a c) -> r a c", a=passes),
                    in_=scales[:, 4 * q : 4 * q + 4, :].bitcast(I32).rearrange("a r c -> r a c"),
                )

        def load_weight(queue, w, a, name):
            raw = held([P, PACK * H], F32, name)
            queue.dma_start(out=raw[:], in_=w[512 * a : 512 * (a + 1), :].rearrange("(p j) c -> p (j c)", j=PACK))
            return raw

        list1 = keep.tile([P, S // 16], U16, name="list1")
        list2 = keep.tile([P, S // 16], U16, name="list2")
        list3 = keep.tile([P, M // 16], U16, name="list3")

        tab_plane = held([P, T], U8, "tab_plane")
        w3_plane_raw = held([P, PASSES * H], U8, "w3_plane_raw")
        v_plane_low = held([P, S], U8, "v_plane_low")
        w4_plane = held([P, N], U8, "w4_plane")
        for plane in (tab_plane, w3_plane_raw, v_plane_low, w4_plane):
            nc.gpsimd.memset(plane[:].bitcast(I32), 0)

        w2_raw = [load_weight(nc.scalar, w2, 0, "w2_raw0")]
        warm = held([P, 2], F32, "warm")
        nc.vector.memset(warm[:, 0:1], 0.0)
        nc.scalar.activation(warm[:, 1:2], warm[:, 0:1], ACT.Silu)
        nc.sync.dma_start(list1[:], offs)
        for q in range(4):
            nc.sync.dma_start(out=tab_plane[32 * q : 32 * q + 8, :].bitcast(I32), in_=tab_scales[:, 4 * q : 4 * q + 4, :].bitcast(I32))
        w3_raw = held([P, PASSES * 2 * H], U8, "w3_raw")
        nc.sync.dma_start(
            out=w3_raw[:].bitcast(I32).rearrange("p (a c) -> p a c", a=PASSES),
            in_=w3_words.bitcast(I32).rearrange("a p c -> p a c"),
        )
        tab_sb = []
        def load_tab(a):
            words = held([P, T], U32, f"tab{a}")
            nc.sync.dma_start(out=words[:].bitcast(I32), in_=tab_words[a].rearrange("p t i -> p (t i)").bitcast(I32))
            tab_sb.append(words)
        load_tab(0)
        b2_sb = held([P, PACK], F32, "b2_sb")
        gain_sb = held([P, PACK], F32, "gain_sb")
        nc.sync.dma_start(out=b2_sb[:], in_=b2.rearrange("(p t) -> p t", t=PACK))
        nc.sync.dma_start(out=gain_sb[:], in_=gain.rearrange("(p t) -> p t", t=PACK))
        load_scale_rows(w3_plane_raw, w3_scales)
        load_tab(1)
        nc.sync.dma_start(list2[:], offs2)
        v_plane = held([P, S], U8, "v_plane")
        nc.vector.tensor_copy(v_plane[:], tab_plane[:].indirect(list1[:]))
        for q in range(4):
            nc.sync.dma_start(out=v_plane_low[32 * q : 32 * q + 4, :].bitcast(I32), in_=v_plane[32 * q + 4 : 32 * q + 8, :].bitcast(I32))
        w2_raw.append(load_weight(nc.sync, w2, 1, "w2_raw1"))
        w1_raw = [load_weight(nc.sync, w1, a, f"w1_raw{a}") for a in range(PASSES)]
        wgs_rows = wgs.rearrange("(q t) j -> q t j", t=PACK)
        page_rows = page0.rearrange("(p t) c -> p t c", t=PACK)
        wgs_sb = [held([P, S], F32, f"wgs{t}") for t in range(PACK)]
        pages = [held([P, T2], F32, f"page{t}") for t in range(PACK)]

        def load_wgs(t, cols):
            for q in range(4):
                nc.sync.dma_start(out=wgs_sb[t][32 * q : 32 * (q + 1), cols], in_=wgs_rows[:, t, cols])

        load_wgs(0, slice(0, HALF))
        nc.sync.dma_start(out=pages[0][:], in_=page_rows[:, 0, :])
        load_wgs(0, slice(HALF, S))
        for t in range(1, PACK - 1):
            nc.sync.dma_start(out=wgs_sb[t][:], in_=wgs_rows[:, t, :].unsqueeze(0).to_broadcast([4, 32, S]))
            nc.sync.dma_start(out=pages[t][:], in_=page_rows[:, t, :])
        nc.sync.dma_start(list3[:], offs3)
        wgt_sb = held([P, M], F32, "wgt_sb")
        nc.sync.dma_start(out=wgt_sb[:], in_=wgt)
        w4_sb = held([P, N], U32, "w4_sb")
        nc.sync.dma_start(out=w4_sb[:].bitcast(I32), in_=w4_words[0].rearrange("p c i -> p (c i)").bitcast(I32))
        load_scale_rows(w4_plane, w4_scales)
        nc.sync.dma_start(out=wgs_sb[PACK - 1][:], in_=wgs_rows[:, PACK - 1, :].unsqueeze(0).to_broadcast([4, 32, S]))
        nc.sync.dma_start(out=pages[PACK - 1][:], in_=page_rows[:, PACK - 1, :])


        w3_sb = held([P, PASSES * 2 * H], U8, "w3_sb")
        w3_plane = held([P, PASSES * H], U8, "w3_plane")
        nc.vector.tensor_copy(
            out=w3_sb[:].bitcast(U16).rearrange("p (a t m) -> p a m t", a=PASSES, t=PACK),
            in_=w3_raw[:].bitcast(U16).rearrange("p (a m t) -> p a m t", a=PASSES, t=PACK),
        )
        nc.vector.tensor_copy(
            out=w3_plane[:].rearrange("p (a t m) -> p a m t", a=PASSES, t=PACK),
            in_=w3_plane_raw[:].rearrange("p (a m t) -> p a m t", a=PASSES, t=PACK),
        )
        turn_bias = held([P, PACK], F32, "turn_bias")
        nc.vector.tensor_scalar(turn_bias[:], b2_sb[:], 1.0 / TWO_PI, 0.25, ALU.mult, ALU.add)

        def quantize(grouped, codes, plane):
            nc.vector.quantize_mx(out=codes[:].bitcast(FP8X4), scales=plane[:], in_=grouped[:])

        def quantize_weight(raw, name, scalar_share):
            grouped = held([P, PACK * H], BF16, name + "_bf")
            dst = grouped[:].rearrange("p (t m j) -> p m t j", t=PACK, j=PACK)
            src = raw[:].rearrange("p (j m t) -> p m t j", j=PACK, t=PACK)
            if scalar_share > 0:
                nc.scalar.copy(out=dst[:, :scalar_share], in_=src[:, :scalar_share])
            if scalar_share < P:
                nc.vector.tensor_copy(out=dst[:, scalar_share:], in_=src[:, scalar_share:])
            codes = held([P, H], U32, name + "_codes")
            plane = held([P, H], U8, name + "_plane")
            quantize(grouped, codes, plane)
            return codes, plane

        def quantize_by_slice(raw, name):
            grouped = held([P, PACK * H], BF16, name + "_bf")
            dst = grouped[:].rearrange("p (t m j) -> p m t j", t=PACK, j=PACK)
            src = raw[:].rearrange("p (j m t) -> p m t j", j=PACK, t=PACK)
            codes = held([P, H], U32, name + "_codes")
            plane = held([P, H], U8, name + "_plane")
            for lo, hi in ((0, 1), (1, PACK)):
                nc.vector.tensor_copy(out=dst[:, :, lo:hi], in_=src[:, :, lo:hi])
                quantize(grouped[:, H * lo : H * hi], codes[:, P * lo : P * hi], plane[:, P * lo : P * hi])
            return codes, plane

        w2_q = [quantize_weight(w2_raw[0], "w2_0", P), quantize_weight(w2_raw[1], "w2_1", 64)]

        v_words = {}
        for half in range(S // HALF):
            for a in range(PASSES):
                words = held([P, HALF], U32, f"v{a}{half}")
                nc.vector.tensor_copy(words[:], tab_sb[a][:].indirect(list1[:, 32 * half : 32 * (half + 1)]))
                v_words[a, half] = words

        def product(bank, stationary, planes, half):
            for a in range(PASSES):
                codes, plane = stationary(a)
                nc.tensor.matmul_mx(
                    out=bank[:], lhsT=codes, lhsT_scale=plane,
                    rhs=v_words[a, half][:].bitcast(FP8X4),
                    rhs_scale=planes[a][:, HALF * half : HALF * (half + 1)],
                    start=(a == 0), stop=(a == PASSES - 1),
                )

        packed_planes = (v_plane[:], v_plane[4:, :])
        low_planes = (v_plane[:], v_plane_low[:])

        def e4m3_slice(quantized, t):
            return lambda a: (quantized[a][0][:, P * t : P * (t + 1)].bitcast(FP8X4), quantized[a][1][:, P * t : P * (t + 1)])

        def w3_slice(t):
            return lambda a: (
                w3_sb[:, 2 * (H * a + P * t) : 2 * (H * a + P * (t + 1))].bitcast(FP4X4),
                w3_plane[:, H * a + P * t : H * a + P * (t + 1)],
            )

        def rotation(pool, dtype, name, count):
            return [pool.tile([P, HALF], dtype, name=f"{name}{i}", tag=f"{name}{i}", bufs=1) for i in range(count)]

        pair_banks = rotation(psum, F32, "pair_bank", 4)
        load_banks = rotation(psum, F32, "load_bank", 3)
        out_banks = rotation(psum, F32, "out_bank", 1) + pair_banks + load_banks
        turns_ring = rotation(ring, F32, "turns", 3)
        whole_ring = rotation(ring, U32, "whole", 3)
        rest_ring = rotation(ring, F32, "rest", 4)
        lean_ring = rotation(ring, F32, "lean", 3)
        wide = [held([P, S + HALF], F32, f"slip{i}") for i in range(4)]
        slip_ring = [tile[:, :HALF] for tile in wide]
        joined_ring = rotation(ring, F32, "joined", 3)
        count_ring = rotation(ring, F32, "count", 2)
        first_weighted = held([P, HALF], F32, "first_weighted")
        units = [(t, half) for t in range(PACK) for half in range(S // HALF)]

        def cosine(i):
            t, half = units[i]
            bank = pair_banks[i % len(pair_banks)]
            product(bank, e4m3_slice(w2_q, t), packed_planes, half)
            turns = turns_ring[i % len(turns_ring)]
            nc.scalar.activation(turns[:], bank[:], ACT.Identity, bias=turn_bias[:, t : t + 1], scale=1.0 / TWO_PI)
            whole = whole_ring[i % len(whole_ring)]
            nc.scalar.activation(whole[:], turns[:], ACT.Copy, bias=ROUNDER, scale=1.0)
            rest = rest_ring[(i if i < len(rest_ring) else i + 1) % len(rest_ring)]
            if i < 3:
                nc.vector.scalar_tensor_tensor(rest[:], whole[:].bitcast(I32), ROUNDER, turns[:], ALU.subtract, ALU.subtract)
            else:
                count = count_ring[i % len(count_ring)]
                nc.scalar.activation(count[:], whole[:], ACT.Copy, bias=-ROUNDER, scale=1.0)
                nc.gpsimd.tensor_tensor(rest[:], count[:], turns[:], ALU.subtract)
            return rest

        leans = [cosine(i) for i in range(1)]
        w1_q = [quantize_weight(w1_raw[0], "w1_0", 48), quantize_by_slice(w1_raw[1], "w1_1")]

        def join(i):
            t, half = units[i]
            slip_bank = pair_banks[i % len(pair_banks)]
            product(slip_bank, e4m3_slice(w1_q, t), packed_planes, half)
            load_bank = load_banks[i % len(load_banks)]
            product(load_bank, w3_slice(t), low_planes, half)
            lean = lean_ring[i % len(lean_ring)]
            nc.scalar.activation(lean[:], leans[i][:], ACT.Sin, scale=-TWO_PI)
            slip = slip_ring[i % len(slip_ring)]
            nc.scalar.activation(slip[:], slip_bank[:], ACT.Tanh)
            joined = joined_ring[i % len(joined_ring)]
            (nc.vector if i < 1 else nc.gpsimd).tensor_tensor(joined[:], slip[:], lean[:], ALU.mult)
            return joined, load_bank

        def add_load(i, joined, load_bank):
            cells = rest_ring[i % len(rest_ring)]
            t = units[i][0]
            nc.vector.scalar_tensor_tensor(cells[:], joined[:], gain_sb[:, t : t + 1], load_bank[:], ALU.mult, ALU.add)
            return cells

        def scatter(i, cells):
            t, half = units[i]
            weighted = slip_ring[(i + 1) % len(slip_ring)] if i > 0 else first_weighted
            (nc.vector if i < 2 else nc.gpsimd).tensor_tensor(weighted[:], cells[:], wgs_sb[t][:, HALF * half : HALF * (half + 1)], ALU.mult)
            nc.vector.tensor_copy(pages[t][:].indirect(list2[:, 32 * half : 32 * (half + 1)]), weighted[:])

        ahead = len(pair_banks)
        cells = [add_load(0, *join(0))]
        leans.extend(cosine(i) for i in range(1, ahead))
        scatter(0, cells[0])
        cells.append(add_load(1, *join(1)))
        for i in range(1, len(units)):
            if i + 1 < len(units):
                cells.append(add_load(i + 1, *join(i + 1)))
            scatter(i, cells[i])
            if i + ahead - 1 < len(units):
                leans.append(cosine(i + ahead - 1))

        stages = (wide[len(units) % len(wide)], wide[(len(units) - 1) % len(wide)])
        out_rows = out.rearrange("(g p) m -> p g m", p=P)
        groups = N // P
        starts = [sum(CHUNKS[:c]) for c in range(len(CHUNKS))]
        last = len(CHUNKS) - 1

        def pick(c):
            width, m0 = CHUNKS[c], starts[c]
            picked = stages[c % 2][:, : PACK * width]
            for t in range(PACK):
                nc.vector.tensor_tensor(
                    picked[:, width * t : width * (t + 1)],
                    pages[t][:].indirect(list3[:, m0 // 16 : (m0 + width) // 16]),
                    wgt_sb[:, m0 : m0 + width], ALU.mult,
                )
            first_word = 3 * CHUNKS[min(c + 1, last)]
            x_bf = stages[(c + 1) % 2][:, first_word : first_word + 2 * width].bitcast(BF16)
            weave = nc.vector.tensor_copy if c >= 3 else nc.scalar.copy
            weave(out=x_bf.rearrange("p (c i t) -> p c t i", i=4, t=PACK), in_=picked.rearrange("p (t c i) -> p c t i", i=4, t=PACK))
            return x_bf

        def features(c, x_codes, x_plane, used):
            width, m0 = CHUNKS[c], starts[c]
            per_bank = 2 if width == 256 else 3
            staged = held([P, groups * width], F32, f"staged{c}", tag=("w2_raw0", "w2_raw1", "tab0", "tab1", "w2_0_bf", "w2_1_bf")[c])
            for b in range(groups // per_bank):
                bank = out_banks[(used + b) % len(out_banks)][:, : per_bank * width]
                for i in range(per_bank):
                    g = per_bank * b + i
                    nc.tensor.matmul_mx(
                        out=bank[:, width * i : width * (i + 1)],
                        lhsT=w4_sb[:, P * g : P * (g + 1)].bitcast(FP8X4), lhsT_scale=w4_plane[:, P * g : P * (g + 1)],
                        rhs=x_codes[:].bitcast(FP8X4), rhs_scale=x_plane[:], start=True, stop=True,
                    )
                part = staged[:, per_bank * width * b : per_bank * width * (b + 1)]
                empty = nc.vector.tensor_copy if (c >= 3 and b == 1) else nc.scalar.copy
                empty(out=part, in_=bank)
                nc.sync.dma_start(
                    out=out_rows[:, per_bank * b : per_bank * (b + 1), m0 : m0 + width],
                    in_=part.rearrange("p (g m) -> p g m", g=per_bank),
                )

        waiting = None
        for c, width in enumerate(CHUNKS):
            x_bf = pick(c)
            if waiting is not None:
                features(c - 1, *waiting, 3 * (c - 1))
            waiting = (held([P, width], U32, f"x_codes{c}"), held([P, width], U8, f"x_plane{c}"))
            quantize(x_bf, *waiting)
        features(last, *waiting, 3 * last)
